import numpy as np
import ml_dtypes


def mxq(x, axis, fmt="e4m3"):
    dtype, down = {"e4m3": (ml_dtypes.float8_e4m3fn, 7), "e5m2": (ml_dtypes.float8_e5m2, 14)}[fmt]
    v = np.moveaxis(np.asarray(x, np.float32).astype(ml_dtypes.bfloat16).astype(np.float64), axis, -1)
    blocks = v.reshape(v.shape[:-1] + (-1, 32))
    amax = np.abs(blocks).max(-1, keepdims=True)
    byte = np.maximum(np.where(amax > 0, np.frexp(amax)[1] - 1 + 127, 0) - down, 1)
    scale = np.exp2(byte - 127.0)
    codes = (blocks / scale).astype(np.float32).astype(dtype).astype(np.float64)
    return np.moveaxis((codes * scale).reshape(v.shape), -1, axis)


WIDE = False


def mx_kscale(k):
    if not WIDE:
        return np.ones(k)
    levels = np.array([10, -10, 5, -5, 0])
    if k % 512:
        return np.exp2(np.random.permutation(np.resize(levels, k // 32))).repeat(32)
    a = np.empty((k // 512, 16))
    for p in range(k // 512):
        a[p, :8] = np.random.permutation(np.resize(levels, 8))
        for g in range(8):
            far = levels[np.abs(levels - a[p, g]) >= 10]
            a[p, g + 8] = far[np.random.randint(len(far))]
    return np.exp2(a.ravel()).repeat(32)


def f64(x):
    return np.asarray(x).astype(np.float64)


def striped(idx):
    return np.tile(np.asarray(idx).reshape(-1, 16).T, (8, 1)).astype(np.uint16)


def unstriped(offs):
    return offs[:16].T.reshape(-1).astype(np.int64)


O, G, T, D, M = 27, 256, 1024, 512, 128


def setup_inputs():
    n = np.random.standard_normal
    s = mx_kscale(D)[:, None]
    x = n((D, T)) * s
    x[:, 0] = 0.0
    idx = np.stack([np.random.permutation(T - 1)[:G] + 1 for o in range(O)])
    idx[np.random.uniform(size=(O, G)) < 0.1] = 0
    return {
        "xT": x.astype(np.float32),
        "w": (n((O, D, M)) / np.sqrt(O * D) / s).astype(np.float32),
        "offs": striped(idx.reshape(-1)),
    }


def reference(xT, w, offs):
    x = f64(xT)[:, unstriped(offs)]
    wq, xq = mxq(f64(w), 1, "e4m3"), mxq(x, 0, "e4m3").reshape(D, O, G)
    y = sum(wq[o].T @ xq[:, o] for o in range(O))
    return y

@@ -1,0 +1,160 @@
+from contextlib import ExitStack
+
+import concourse.mybir as mybir
+
+TAPS, SITES, COLS, D, M = 27, 256, 1024, 512, 128
+P = 128
+FLOPS = 2 * TAPS * SITES * D * M
+
+F32 = mybir.dt.float32
+BF16 = mybir.dt.bfloat16
+U32 = mybir.dt.uint32
+U16 = mybir.dt.uint16
+U8 = mybir.dt.uint8
+FP8X4 = mybir.dt.float8_e4m3fn_x4
+COPY = mybir.ActivationFunctionType.Copy
+
+W_LOADS = (2, 2, 4, 4, 4, 4, 4, 3)
+W_GROUPS = (2, 2, 4, 4, 4, 4, 4, 2, 1)
+X_CHUNKS = (2,) * 13 + (1,)
+
+
+def starts(sizes):
+    return [sum(sizes[:i]) for i in range(len(sizes))]
+
+
+def tile_attend_spconv_kernel(tc, xT, w, offs, out):
+    nc = tc.nc
+    with ExitStack() as ctx:
+        keep = ctx.enter_context(tc.tile_pool(name="keep", bufs=1))
+        ring = ctx.enter_context(tc.tile_pool(name="ring", bufs=4))
+        psum = ctx.enter_context(tc.psum_pool(name="psum", bufs=1))
+
+        offsets = keep.tile([P, TAPS * SITES // 16], U16, name="offsets")
+        nc.sync.dma_start(offsets[:], offs)
+
+        x_rows = xT.rearrange("(p t) c -> p t c", t=4)
+        pool_words = []
+        half = COLS // 2
+        raws = {}
+        for h in range(2):
+            for q in range(2):
+                raw = keep.tile([P, 2, half], F32, name=f"xraw{h}{q}")
+                nc.sync.dma_start(raw[:], x_rows[:, 2 * h : 2 * h + 2, q * half : (q + 1) * half])
+                raws[(h, q)] = raw
+        w_raw = {}
+        for i, (o0, n) in enumerate(zip(starts(W_LOADS), W_LOADS)):
+            raw = keep.tile([P, n, 4, M], F32, name=f"wraw{i}")
+            nc.sync.dma_start(raw[:], w[o0 : o0 + n].rearrange("o (p t) m -> p o t m", t=4))
+            for j in range(n):
+                w_raw[o0 + j] = raw[:, j]
+
+        for h in range(2):
+            pair = keep.tile([P, COLS, 2], BF16, name=f"pool{h}", align_bytes=64)
+            for q in range(2):
+                dst = pair[:, q * half : (q + 1) * half, :]
+                src = raws[(h, q)][:].rearrange("p e c -> p c e")
+                if h == 0 and q == 1:
+                    nc.vector.tensor_copy(dst, src)
+                else:
+                    nc.scalar.activation(dst, src, COPY)
+            pool_words.append(pair[:].rearrange("p c e -> p (c e)").bitcast(U32))
+
+        acc = psum.tile([M, SITES], F32)
+
+        w_codes, x_codes = {}, {}
+        w_queue = list(zip(starts(W_GROUPS), W_GROUPS))
+
+        def cast_w(o0, n):
+            grouped = ring.tile([P, n, M, 4], BF16, name="wg", align_bytes=64)
+            for j in range(n):
+                nc.scalar.activation(
+                    grouped[:, j].rearrange("p (c i) t -> p c t i", i=4),
+                    w_raw[o0 + j].rearrange("p t (c i) -> p c t i", i=4),
+                    COPY,
+                )
+            return grouped
+
+        def quant_w(o0, n, grouped):
+            codes = keep.tile([P, n * M], U32, name=f"wc{o0}", align_bytes=64)
+            scales = keep.tile([P, n * M], U8, name=f"ws{o0}", align_bytes=64)
+            nc.vector.quantize_mx(
+                out=codes[:].bitcast(FP8X4),
+                scales=scales[:],
+                in_=grouped[:].rearrange("p o m t -> p (o m t)"),
+            )
+            for j in range(n):
+                w_codes[o0 + j] = (codes[:, j * M : (j + 1) * M], scales[:, j * M : (j + 1) * M])
+
+        def gather(o0, n):
+            cols = n * SITES
+            first = o0 * SITES // 16
+            planes = ring.tile([P, 2, cols], U32, name="planes", align_bytes=64)
+            for h in range(2):
+                nc.vector.tensor_copy(
+                    planes[:, h, :],
+                    pool_words[h].indirect(offsets[:, first : first + cols // 16]),
+                )
+            return planes
+
+        def interleave(n, planes):
+            grouped = ring.tile([P, n * SITES, 2], U32, name="xg", align_bytes=64)
+            nc.scalar.copy(grouped[:], planes[:].rearrange("p h c -> p c h"))
+            return grouped
+
+        def quant_x(o0, n, grouped):
+            cols = n * SITES
+            codes = ring.tile([P, cols], U32, name="xc", align_bytes=64)
+            scales = ring.tile([P, cols], U8, name="xs", align_bytes=64)
+            nc.vector.quantize_mx(
+                out=codes[:].bitcast(FP8X4),
+                scales=scales[:],
+                in_=grouped[:].rearrange("p c h -> p (c h)").bitcast(BF16),
+            )
+            for j in range(n):
+                x_codes[o0 + j] = (codes[:, j * SITES : (j + 1) * SITES], scales[:, j * SITES : (j + 1) * SITES])
+
+        def multiply(o):
+            wc, ws = w_codes[o]
+            xc, xs = x_codes[o]
+            nc.tensor.matmul_mx(
+                out=acc[:],
+                lhsT=wc.bitcast(FP8X4),
+                lhsT_scale=ws,
+                rhs=xc.bitcast(FP8X4),
+                rhs_scale=xs,
+                start=(o == 0),
+                stop=(o == TAPS - 1),
+            )
+
+        x_list = list(zip(starts(X_CHUNKS), X_CHUNKS))
+        planes, grouped, w_grouped = {}, {}, {}
+        w_cast = 0
+        w_quant = 0
+        done = 0
+        for i in range(len(x_list) + 2):
+            if i < len(x_list):
+                planes[i] = gather(*x_list[i])
+                grouped[i] = interleave(x_list[i][1], planes[i])
+            if 1 <= i < len(x_list) + 1:
+                quant_x(*x_list[i - 1], grouped[i - 1])
+            limit = min(TAPS, 2 * (i + 1))
+            while w_cast < len(w_queue) and w_queue[w_cast][0] < limit:
+                w_grouped[w_cast] = cast_w(*w_queue[w_cast])
+                w_cast += 1
+            while w_quant < len(w_queue) and w_queue[w_quant][0] < limit - 2:
+                quant_w(*w_queue[w_quant], w_grouped[w_quant])
+                w_quant += 1
+            while done < TAPS and done in w_codes and done in x_codes and done < 2 * (i - 1):
+                multiply(done)
+                done += 1
+        while w_quant < len(w_queue):
+            quant_w(*w_queue[w_quant], w_grouped[w_quant])
+            w_quant += 1
+        while done < TAPS:
+            multiply(done)
+            done += 1
+
+        result = keep.tile([M, SITES], F32, name="result")
+        nc.vector.tensor_copy(result[:], acc[:])
+        nc.sync.dma_start(out, result[:])

@@ -15,8 +15,11 @@ FP8X4 = mybir.dt.float8_e4m3fn_x4
 COPY = mybir.ActivationFunctionType.Copy
 
 W_LOADS = (2, 2, 4, 4, 4, 4, 4, 3)
-W_GROUPS = (2, 2, 4, 4, 4, 4, 4, 2, 1)
-X_CHUNKS = (2,) * 13 + (1,)
+W_GROUPS = (2,) * 13 + (1,)
+X_CHUNKS = (512,) * 12 + (256, 256, 128, 128)
+HALF = 128
+A_SPLIT = ((0, 640, 400), (640, 1024, 240))
+B_SPLIT = ((0, 512), (512, 1024))
 
 
 def starts(sizes):
@@ -28,20 +31,20 @@ def tile_attend_spconv_kernel(tc, xT, w, offs, out):
     with ExitStack() as ctx:
         keep = ctx.enter_context(tc.tile_pool(name="keep", bufs=1))
         ring = ctx.enter_context(tc.tile_pool(name="ring", bufs=4))
+        wring = ctx.enter_context(tc.tile_pool(name="wring", bufs=3))
         psum = ctx.enter_context(tc.psum_pool(name="psum", bufs=1))
 
+        x_rows = xT.rearrange("(p t) c -> p t c", t=4)
+
+        def load_x(h, c0, c1):
+            raw = keep.tile([P, 2, c1 - c0], F32, name=f"xraw{h}_{c0}")
+            nc.sync.dma_start(raw[:], x_rows[:, 2 * h : 2 * h + 2, c0:c1])
+            return raw[:].rearrange("p e c -> p c e")
+
+        a_raw = [load_x(0, c0, c1) for c0, c1, n in A_SPLIT]
         offsets = keep.tile([P, TAPS * SITES // 16], U16, name="offsets")
         nc.sync.dma_start(offsets[:], offs)
-
-        x_rows = xT.rearrange("(p t) c -> p t c", t=4)
-        pool_words = []
-        half = COLS // 2
-        raws = {}
-        for h in range(2):
-            for q in range(2):
-                raw = keep.tile([P, 2, half], F32, name=f"xraw{h}{q}")
-                nc.sync.dma_start(raw[:], x_rows[:, 2 * h : 2 * h + 2, q * half : (q + 1) * half])
-                raws[(h, q)] = raw
+        b_raw = [load_x(1, c0, c1) for c0, c1 in B_SPLIT]
         w_raw = {}
         for i, (o0, n) in enumerate(zip(starts(W_LOADS), W_LOADS)):
             raw = keep.tile([P, n, 4, M], F32, name=f"wraw{i}")
@@ -49,24 +52,20 @@ def tile_attend_spconv_kernel(tc, xT, w, offs, out):
             for j in range(n):
                 w_raw[o0 + j] = raw[:, j]
 
-        for h in range(2):
-            pair = keep.tile([P, COLS, 2], BF16, name=f"pool{h}", align_bytes=64)
-            for q in range(2):
-                dst = pair[:, q * half : (q + 1) * half, :]
-                src = raws[(h, q)][:].rearrange("p e c -> p c e")
-                if h == 0 and q == 1:
-                    nc.vector.tensor_copy(dst, src)
-                else:
-                    nc.scalar.activation(dst, src, COPY)
-            pool_words.append(pair[:].rearrange("p c e -> p (c e)").bitcast(U32))
+        pool_a = keep.tile([P, COLS, 2], BF16, align_bytes=64)
+        pool_b = keep.tile([P, COLS, 2], BF16, align_bytes=64)
+        for (c0, c1, n), src in zip(A_SPLIT, a_raw):
+            nc.vector.tensor_copy(pool_a[:, c0 : c0 + n, :], src[:, :n, :])
+            nc.scalar.activation(pool_a[:, c0 + n : c1, :], src[:, n:, :], COPY)
+        for (c0, c1), src in zip(B_SPLIT, b_raw):
+            nc.scalar.activation(pool_b[:, c0:c1, :], src, COPY)
+        windows = [t[:].rearrange("p c e -> p (c e)").bitcast(U32) for t in (pool_a, pool_b)]
 
-        acc = psum.tile([M, SITES], F32)
-
+        accs = [psum.tile([M, HALF], F32, name=f"acc{s}") for s in range(2)]
         w_codes, x_codes = {}, {}
-        w_queue = list(zip(starts(W_GROUPS), W_GROUPS))
 
         def cast_w(o0, n):
-            grouped = ring.tile([P, n, M, 4], BF16, name="wg", align_bytes=64)
+            grouped = wring.tile([P, n, M, 4], BF16, name="wg", align_bytes=64)
             for j in range(n):
                 nc.scalar.activation(
                     grouped[:, j].rearrange("p (c i) t -> p c t i", i=4),
@@ -75,86 +74,66 @@ def tile_attend_spconv_kernel(tc, xT, w, offs, out):
                 )
             return grouped
 
-        def quant_w(o0, n, grouped):
-            codes = keep.tile([P, n * M], U32, name=f"wc{o0}", align_bytes=64)
-            scales = keep.tile([P, n * M], U8, name=f"ws{o0}", align_bytes=64)
-            nc.vector.quantize_mx(
-                out=codes[:].bitcast(FP8X4),
-                scales=scales[:],
-                in_=grouped[:].rearrange("p o m t -> p (o m t)"),
-            )
-            for j in range(n):
-                w_codes[o0 + j] = (codes[:, j * M : (j + 1) * M], scales[:, j * M : (j + 1) * M])
+        def quantise(tag, bf16_cols, width):
+            codes = keep.tile([P, width], U32, name=tag + "c", align_bytes=64)
+            scales = keep.tile([P, width], U8, name=tag + "s", align_bytes=64)
+            nc.vector.quantize_mx(out=codes[:].bitcast(FP8X4), scales=scales[:], in_=bf16_cols)
+            return codes, scales
 
-        def gather(o0, n):
-            cols = n * SITES
-            first = o0 * SITES // 16
+        def gather(c0, cols):
             planes = ring.tile([P, 2, cols], U32, name="planes", align_bytes=64)
             for h in range(2):
                 nc.vector.tensor_copy(
                     planes[:, h, :],
-                    pool_words[h].indirect(offsets[:, first : first + cols // 16]),
+                    windows[h].indirect(offsets[:, c0 // 16 : (c0 + cols) // 16]),
                 )
             return planes
 
-        def interleave(n, planes):
-            grouped = ring.tile([P, n * SITES, 2], U32, name="xg", align_bytes=64)
+        def interleave(cols, planes):
+            grouped = ring.tile([P, cols, 2], U32, name="xg", align_bytes=64)
             nc.scalar.copy(grouped[:], planes[:].rearrange("p h c -> p c h"))
             return grouped
 
-        def quant_x(o0, n, grouped):
-            cols = n * SITES
-            codes = ring.tile([P, cols], U32, name="xc", align_bytes=64)
-            scales = ring.tile([P, cols], U8, name="xs", align_bytes=64)
-            nc.vector.quantize_mx(
-                out=codes[:].bitcast(FP8X4),
-                scales=scales[:],
-                in_=grouped[:].rearrange("p c h -> p (c h)").bitcast(BF16),
-            )
-            for j in range(n):
-                x_codes[o0 + j] = (codes[:, j * SITES : (j + 1) * SITES], scales[:, j * SITES : (j + 1) * SITES])
+        def multiply(k, c0, cols):
+            xc, xs = x_codes[k]
+            for c in range(0, cols, HALF):
+                o, side = (c0 + c) // SITES, (c0 + c) % SITES // HALF
+                wc, ws = w_codes[o // 2]
+                m0 = o % 2 * M
+                nc.tensor.matmul_mx(
+                    out=accs[side][:],
+                    lhsT=wc[:, m0 : m0 + M].bitcast(FP8X4),
+                    lhsT_scale=ws[:, m0 : m0 + M],
+                    rhs=xc[:, c : c + HALF].bitcast(FP8X4),
+                    rhs_scale=xs[:, c : c + HALF],
+                    start=(o == 0),
+                    stop=(o == TAPS - 1),
+                )
 
-        def multiply(o):
-            wc, ws = w_codes[o]
-            xc, xs = x_codes[o]
-            nc.tensor.matmul_mx(
-                out=acc[:],
-                lhsT=wc.bitcast(FP8X4),
-                lhsT_scale=ws,
-                rhs=xc.bitcast(FP8X4),
-                rhs_scale=xs,
-                start=(o == 0),
-                stop=(o == TAPS - 1),
-            )
+        groups = list(zip(starts(W_GROUPS), W_GROUPS))
+        chunks = list(zip(starts(X_CHUNKS), X_CHUNKS))
+        steps = len(chunks)
+        planes, x_grouped, w_grouped = {}, {}, {}
+        for i in range(steps + 3):
+            if i < steps:
+                planes[i] = gather(*chunks[i])
+                x_grouped[i] = interleave(chunks[i][1], planes[i])
+            for k in range(len(groups)):
+                if k * 6 // 7 == i:
+                    w_grouped[k] = cast_w(*groups[k])
+            if 2 <= i < steps + 2:
+                k = i - 2
+                x_codes[k] = quantise(f"x{k}", x_grouped[k][:].rearrange("p c h -> p (c h)").bitcast(BF16), chunks[k][1])
+            for k in range(len(groups)):
+                if k * 6 // 7 + 2 == i:
+                    w_codes[k] = quantise(f"w{k}", w_grouped[k][:].rearrange("p o m t -> p (o m t)"), groups[k][1] * M)
+            if i >= 3:
+                multiply(i - 3, *chunks[i - 3])
 
-        x_list = list(zip(starts(X_CHUNKS), X_CHUNKS))
-        planes, grouped, w_grouped = {}, {}, {}
-        w_cast = 0
-        w_quant = 0
-        done = 0
-        for i in range(len(x_list) + 2):
-            if i < len(x_list):
-                planes[i] = gather(*x_list[i])
-                grouped[i] = interleave(x_list[i][1], planes[i])
-            if 1 <= i < len(x_list) + 1:
-                quant_x(*x_list[i - 1], grouped[i - 1])
-            limit = min(TAPS, 2 * (i + 1))
-            while w_cast < len(w_queue) and w_queue[w_cast][0] < limit:
-                w_grouped[w_cast] = cast_w(*w_queue[w_cast])
-                w_cast += 1
-            while w_quant < len(w_queue) and w_queue[w_quant][0] < limit - 2:
-                quant_w(*w_queue[w_quant], w_grouped[w_quant])
-                w_quant += 1
-            while done < TAPS and done in w_codes and done in x_codes and done < 2 * (i - 1):
-                multiply(done)
-                done += 1
-        while w_quant < len(w_queue):
-            quant_w(*w_queue[w_quant], w_grouped[w_quant])
-            w_quant += 1
-        while done < TAPS:
-            multiply(done)
-            done += 1
-
-        result = keep.tile([M, SITES], F32, name="result")
-        nc.vector.tensor_copy(result[:], acc[:])
-        nc.sync.dma_start(out, result[:])
+        for side in range(2):
+            result = keep.tile([M, HALF], F32, name=f"result{side}")
+            if side == 0:
+                nc.scalar.copy(result[:], accs[side][:])
+            else:
+                nc.vector.tensor_copy(result[:], accs[side][:])
+            nc.sync.dma_start(out[:, side * HALF : (side + 1) * HALF], result[:])

from contextlib import ExitStack

import concourse.mybir as mybir

TAPS, SITES, COLS, D, M = 27, 256, 1024, 512, 128
P = 128
FLOPS = 2 * TAPS * SITES * D * M

F32 = mybir.dt.float32
BF16 = mybir.dt.bfloat16
U32 = mybir.dt.uint32
U16 = mybir.dt.uint16
U8 = mybir.dt.uint8
FP8X4 = mybir.dt.float8_e4m3fn_x4
COPY = mybir.ActivationFunctionType.Copy

W_LOADS = (2, 2, 4, 4, 4, 4, 4, 3)
W_GROUPS = (2,) * 13 + (1,)
X_CHUNKS = (512,) * 12 + (256, 256, 128, 128)
HALF = 128
A_SPLIT = ((0, 640, 400), (640, 1024, 240))
B_SPLIT = ((0, 512), (512, 1024))


def starts(sizes):
    return [sum(sizes[:i]) for i in range(len(sizes))]


def tile_attend_spconv_kernel(tc, xT, w, offs, out):
    nc = tc.nc
    with ExitStack() as ctx:
        keep = ctx.enter_context(tc.tile_pool(name="keep", bufs=1))
        ring = ctx.enter_context(tc.tile_pool(name="ring", bufs=4))
        wring = ctx.enter_context(tc.tile_pool(name="wring", bufs=3))
        psum = ctx.enter_context(tc.psum_pool(name="psum", bufs=1))

        x_rows = xT.rearrange("(p t) c -> p t c", t=4)

        def load_x(h, c0, c1):
            raw = keep.tile([P, 2, c1 - c0], F32, name=f"xraw{h}_{c0}")
            nc.sync.dma_start(raw[:], x_rows[:, 2 * h : 2 * h + 2, c0:c1])
            return raw[:].rearrange("p e c -> p c e")

        a_raw = [load_x(0, c0, c1) for c0, c1, n in A_SPLIT]
        offsets = keep.tile([P, TAPS * SITES // 16], U16, name="offsets")
        nc.sync.dma_start(offsets[:], offs)
        b_raw = [load_x(1, c0, c1) for c0, c1 in B_SPLIT]
        w_raw = {}
        for i, (o0, n) in enumerate(zip(starts(W_LOADS), W_LOADS)):
            raw = keep.tile([P, n, 4, M], F32, name=f"wraw{i}")
            nc.sync.dma_start(raw[:], w[o0 : o0 + n].rearrange("o (p t) m -> p o t m", t=4))
            for j in range(n):
                w_raw[o0 + j] = raw[:, j]

        pool_a = keep.tile([P, COLS, 2], BF16, align_bytes=64)
        pool_b = keep.tile([P, COLS, 2], BF16, align_bytes=64)
        for (c0, c1, n), src in zip(A_SPLIT, a_raw):
            nc.vector.tensor_copy(pool_a[:, c0 : c0 + n, :], src[:, :n, :])
            nc.scalar.activation(pool_a[:, c0 + n : c1, :], src[:, n:, :], COPY)
        for (c0, c1), src in zip(B_SPLIT, b_raw):
            nc.scalar.activation(pool_b[:, c0:c1, :], src, COPY)
        windows = [t[:].rearrange("p c e -> p (c e)").bitcast(U32) for t in (pool_a, pool_b)]

        accs = [psum.tile([M, HALF], F32, name=f"acc{s}") for s in range(2)]
        w_codes, x_codes = {}, {}

        def cast_w(o0, n):
            grouped = wring.tile([P, n, M, 4], BF16, name="wg", align_bytes=64)
            for j in range(n):
                nc.scalar.activation(
                    grouped[:, j].rearrange("p (c i) t -> p c t i", i=4),
                    w_raw[o0 + j].rearrange("p t (c i) -> p c t i", i=4),
                    COPY,
                )
            return grouped

        def quantise(tag, bf16_cols, width):
            codes = keep.tile([P, width], U32, name=tag + "c", align_bytes=64)
            scales = keep.tile([P, width], U8, name=tag + "s", align_bytes=64)
            nc.vector.quantize_mx(out=codes[:].bitcast(FP8X4), scales=scales[:], in_=bf16_cols)
            return codes, scales

        def gather(c0, cols):
            planes = ring.tile([P, 2, cols], U32, name="planes", align_bytes=64)
            for h in range(2):
                nc.vector.tensor_copy(
                    planes[:, h, :],
                    windows[h].indirect(offsets[:, c0 // 16 : (c0 + cols) // 16]),
                )
            return planes

        def interleave(cols, planes):
            grouped = ring.tile([P, cols, 2], U32, name="xg", align_bytes=64)
            nc.scalar.copy(grouped[:], planes[:].rearrange("p h c -> p c h"))
            return grouped

        def multiply(k, c0, cols):
            xc, xs = x_codes[k]
            for c in range(0, cols, HALF):
                o, side = (c0 + c) // SITES, (c0 + c) % SITES // HALF
                wc, ws = w_codes[o // 2]
                m0 = o % 2 * M
                nc.tensor.matmul_mx(
                    out=accs[side][:],
                    lhsT=wc[:, m0 : m0 + M].bitcast(FP8X4),
                    lhsT_scale=ws[:, m0 : m0 + M],
                    rhs=xc[:, c : c + HALF].bitcast(FP8X4),
                    rhs_scale=xs[:, c : c + HALF],
                    start=(o == 0),
                    stop=(o == TAPS - 1),
                )

        groups = list(zip(starts(W_GROUPS), W_GROUPS))
        chunks = list(zip(starts(X_CHUNKS), X_CHUNKS))
        steps = len(chunks)
        planes, x_grouped, w_grouped = {}, {}, {}
        for i in range(steps + 3):
            if i < steps:
                planes[i] = gather(*chunks[i])
                x_grouped[i] = interleave(chunks[i][1], planes[i])
            for k in range(len(groups)):
                if k * 6 // 7 == i:
                    w_grouped[k] = cast_w(*groups[k])
            if 2 <= i < steps + 2:
                k = i - 2
                x_codes[k] = quantise(f"x{k}", x_grouped[k][:].rearrange("p c h -> p (c h)").bitcast(BF16), chunks[k][1])
            for k in range(len(groups)):
                if k * 6 // 7 + 2 == i:
                    w_codes[k] = quantise(f"w{k}", w_grouped[k][:].rearrange("p o m t -> p (o m t)"), groups[k][1] * M)
            if i >= 3:
                multiply(i - 3, *chunks[i - 3])

        for side in range(2):
            result = keep.tile([M, HALF], F32, name=f"result{side}")
            if side == 0:
                nc.scalar.copy(result[:], accs[side][:])
            else:
                nc.vector.tensor_copy(result[:], accs[side][:])
            nc.sync.dma_start(out[:, side * HALF : (side + 1) * HALF], result[:])
